import numpy as np
import ml_dtypes


def mxq(x, axis, fmt="e4m3"):
    dtype, down = {"e4m3": (ml_dtypes.float8_e4m3fn, 7), "e5m2": (ml_dtypes.float8_e5m2, 14)}[fmt]
    v = np.moveaxis(np.asarray(x, np.float32).astype(ml_dtypes.bfloat16).astype(np.float64), axis, -1)
    blocks = v.reshape(v.shape[:-1] + (-1, 32))
    amax = np.abs(blocks).max(-1, keepdims=True)
    byte = np.maximum(np.where(amax > 0, np.frexp(amax)[1] - 1 + 127, 0) - down, 1)
    scale = np.exp2(byte - 127.0)
    codes = (blocks / scale).astype(np.float32).astype(dtype).astype(np.float64)
    return np.moveaxis((codes * scale).reshape(v.shape), -1, axis)


WIDE = False


def mx_kscale(k):
    if not WIDE:
        return np.ones(k)
    levels = np.array([10, -10, 5, -5, 0])
    if k % 512:
        return np.exp2(np.random.permutation(np.resize(levels, k // 32))).repeat(32)
    a = np.empty((k // 512, 16))
    for p in range(k // 512):
        a[p, :8] = np.random.permutation(np.resize(levels, 8))
        for g in range(8):
            far = levels[np.abs(levels - a[p, g]) >= 10]
            a[p, g + 8] = far[np.random.randint(len(far))]
    return np.exp2(a.ravel()).repeat(32)


def f64(x):
    return np.asarray(x).astype(np.float64)


E2M1 = np.array([0.0, 0.5, 1.0, 1.5, 2.0, 3.0, 4.0, 6.0, -0.0, -0.5, -1.0, -1.5, -2.0, -3.0, -4.0, -6.0])


def pack_weight(w, fmt):
    k, n = w.shape
    w = f64(np.asarray(w, np.float32).astype(ml_dtypes.bfloat16)).reshape(k // 32, 32, n)
    amax = np.abs(w).max(1)
    if fmt == "e4m3":
        byte = np.frexp(amax)[1] - 1 + 127 - 7
    else:
        mant, ex = np.frexp(amax / 6.0)
        byte = np.where(mant > 0.5, ex, ex - 1) + 127
    byte = np.clip(np.where(amax > 0, byte, 1), 1, 254)
    scaled = (w * np.exp2(127.0 - byte)[:, None, :]).reshape(k, n).astype(np.float32)
    by_word = np.ascontiguousarray(scaled.reshape(k // 512, 128, 4, n).transpose(0, 1, 3, 2))
    if fmt == "e4m3":
        words = by_word.astype(ml_dtypes.float8_e4m3fn).view(np.uint8)
    else:
        c = by_word.astype(ml_dtypes.float4_e2m1fn).view(np.uint8) & 0xF
        words = (c[..., 0::2] | (c[..., 1::2] << 4)).reshape(k // 512, 128, 2 * n)
    return np.ascontiguousarray(words), np.ascontiguousarray(byte.astype(np.uint8).reshape(k // 512, 16, n))


def unpack_weight(words, scales, fmt):
    g, _, n = scales.shape
    words = np.ascontiguousarray(words).reshape(g, 128, n, -1)
    if fmt == "e4m3":
        vals = words.view(ml_dtypes.float8_e4m3fn).astype(np.float64)
    else:
        nib = np.empty((g, 128, n, 4), np.uint8)
        nib[..., 0::2] = words & 0xF
        nib[..., 1::2] = words >> 4
        vals = E2M1[nib]
    vals = vals * np.repeat(np.exp2(scales.astype(np.float64) - 127.0), 8, axis=1)[..., None]
    return vals.transpose(0, 1, 3, 2).reshape(g * 512, n)


O, K, M, T = 512, 1024, 1024, 1024


def setup_inputs():
    n = np.random.standard_normal
    s = mx_kscale(K)[:, None]
    x = n((K, T)); x[:O] *= 6.0
    w = n((K, M)) / np.sqrt(K) / s; w[:O] /= 2.0
    p_w8 = pack_weight(w[:O], "e4m3")
    p_w4 = pack_weight(w[O:], "e2m1")
    return {
        "x": (x * s).astype(np.float32),
        "w8_words": p_w8[0],
        "w8_scales": p_w8[1],
        "w4_words": p_w4[0],
        "w4_scales": p_w4[1],
        "r": (n((1024, 1024))).astype(np.float32),
    }


def reference(x, w8_words, w8_scales, w4_words, w4_scales, r):
    x_ = mxq(f64(x), 0, "e4m3")
    w8_ = unpack_weight(w8_words, w8_scales, "e4m3")
    w4_ = unpack_weight(w4_words, w4_scales, "e2m1")
    y = x_[:O].T @ w8_ + x_[O:].T @ w4_
    return f64(r) + y

@@ -1,0 +1,151 @@
+from contextlib import ExitStack
+
+import concourse.mybir as mybir
+
+O, K, N, T = 512, 1024, 1024, 1024
+FLOPS = 2 * K * N * T
+
+F32 = mybir.dt.float32
+BF16 = mybir.dt.bfloat16
+I32 = mybir.dt.int32
+U32 = mybir.dt.uint32
+U8 = mybir.dt.uint8
+FP8X4 = mybir.dt.float8_e4m3fn_x4
+FP4X4 = mybir.dt.float4_e2m1fn_x4
+
+P = 128
+PACK = 4
+K_PASS = P * PACK
+PAIR = 2
+CHUNK = PAIR * P
+N_CHUNKS = T // CHUNK
+N_BANK = 512
+N_HALVES = N // N_BANK
+Q_ROWS = 4
+
+
+def tile_mix_outl_tm_res_kernel(
+    tc, x, w8_words, w8_scales, w4_words, w4_scales, r, out
+):
+    nc = tc.nc
+    with ExitStack() as ctx:
+        keep = ctx.enter_context(tc.tile_pool(name="keep", bufs=1))
+        psum = ctx.enter_context(tc.psum_pool(name="psum", bufs=8))
+        ctx.enter_context(tc.manual_schedule())
+
+        x_raw = []
+        for g in range(K // K_PASS):
+            raw = keep.tile([P, PACK, T], F32, name="x_raw%d" % g, align_bytes=64)
+            x_raw.append(raw)
+        w8 = keep.tile([P, 4 * N], U8, name="w8", align_bytes=64)
+        w4 = keep.tile([P, 2 * N], U8, name="w4", align_bytes=64)
+        w8_plane = keep.tile([P, N], U8, name="w8_plane", align_bytes=64)
+        w4_plane = keep.tile([P, N], U8, name="w4_plane", align_bytes=64)
+
+        def load_x(g):
+            nc.sync.dma_start(
+                out=x_raw[g][:].rearrange("p k t -> p (k t)"),
+                in_=x[g * K_PASS : (g + 1) * K_PASS, :].rearrange("(p k) t -> p (k t)", k=PACK),
+            )
+
+        load_x(0)
+        nc.sync.dma_start(
+            out=w8[:].bitcast(I32), in_=w8_words[0].rearrange("p n i -> p (n i)").bitcast(I32)
+        )
+        nc.sync.dma_start(out=w4[:].bitcast(I32), in_=w4_words[0].bitcast(I32))
+        load_x(1)
+        r_in = []
+        for c in range(N_CHUNKS):
+            rt = keep.tile([P, PAIR, N], F32, name="r%d" % c, align_bytes=64)
+            r_in.append(rt)
+            nc.sync.dma_start(
+                out=rt[:].rearrange("p e n -> p (e n)"),
+                in_=r[c * CHUNK : (c + 1) * CHUNK, :].rearrange("(p e) n -> p (e n)", e=PAIR),
+            )
+
+        for plane, scales in ((w8_plane, w8_scales), (w4_plane, w4_scales)):
+            nc.vector.memset(plane[:].bitcast(I32), 0)
+            for q in range(P // 32):
+                nc.gpsimd.dma_start(
+                    out=plane[32 * q : 32 * q + Q_ROWS, :].bitcast(I32),
+                    in_=scales[0, Q_ROWS * q : Q_ROWS * (q + 1), :].bitcast(I32),
+                )
+
+        x_codes = {}
+        x_planes = {}
+        grouped = {}
+        for g in range(2):
+            for c in range(N_CHUNKS):
+                t_g = keep.tile([P, CHUNK * PACK], BF16, name="grouped%d_%d" % (g, c), align_bytes=64)
+                t_c = keep.tile([P, CHUNK], U32, name="codes%d_%d" % (g, c), align_bytes=64)
+                t_s = keep.tile([P, CHUNK], U8, name="xscale%d_%d" % (g, c), align_bytes=64)
+                grouped[g, c] = t_g
+                x_codes[g, c] = t_c
+                x_planes[g, c] = t_s
+
+        def regroup(g, c, copy):
+            copy(
+                out=grouped[g, c][:].rearrange("p (e m k) -> p e m k", e=PAIR, k=PACK),
+                in_=x_raw[g][:, :, c * CHUNK : (c + 1) * CHUNK].rearrange(
+                    "p k (m e) -> p e m k", e=PAIR
+                ),
+            )
+
+        def quantize(g, c):
+            nc.vector.quantize_mx(
+                out=x_codes[g, c][:].bitcast(FP8X4), scales=x_planes[g, c][:], in_=grouped[g, c][:]
+            )
+
+        for g in range(2):
+            regroup(g, 0, nc.vector.tensor_copy)
+            regroup(g, 2, nc.scalar.copy)
+            regroup(g, 1, nc.vector.tensor_copy)
+            regroup(g, 3, nc.scalar.copy)
+            for c in range(N_CHUNKS):
+                quantize(g, c)
+
+        banks = {}
+
+        def first_pass(c, e, h):
+            acc = psum.tile([P, N_BANK], F32, name="acc")
+            banks[c, e, h] = acc
+            nc.tensor.matmul_mx(
+                out=acc[:],
+                lhsT=x_codes[0, c][:, e * P : (e + 1) * P].bitcast(FP8X4),
+                lhsT_scale=x_planes[0, c][:, e * P : (e + 1) * P],
+                rhs=w8[:, 4 * N_BANK * h : 4 * N_BANK * (h + 1)].bitcast(FP8X4),
+                rhs_scale=w8_plane[:, N_BANK * h : N_BANK * (h + 1)],
+                start=True,
+                stop=False,
+            )
+
+        def second_pass(c, e, h):
+            nc.tensor.matmul_mx(
+                out=banks[c, e, h][:],
+                lhsT=x_codes[1, c][:, e * P : (e + 1) * P].bitcast(FP8X4),
+                lhsT_scale=x_planes[1, c][:, e * P : (e + 1) * P],
+                rhs=w4[:, 2 * N_BANK * h : 2 * N_BANK * (h + 1)].bitcast(FP4X4),
+                rhs_scale=w4_plane[:, N_BANK * h : N_BANK * (h + 1)],
+                start=False,
+                stop=True,
+            )
+
+        places = [(e, h) for e in range(PAIR) for h in range(N_HALVES)]
+        for c in range(2):
+            for e, h in places:
+                first_pass(c, e, h)
+        for c in range(N_CHUNKS):
+            for e, h in places:
+                if c >= 2:
+                    first_pass(c, e, h)
+                second_pass(c, e, h)
+            res = keep.tile([P, PAIR, N], F32, name="res%d" % c, align_bytes=64)
+            for e, h in places:
+                cols = slice(N_BANK * h, N_BANK * (h + 1))
+                nc.vector.tensor_add(
+                    out=res[:, e, cols], in0=banks[c, e, h][:], in1=r_in[c][:, e, cols]
+                )
+            nc.sync.dma_start(
+                out=out[c * CHUNK : (c + 1) * CHUNK, :].rearrange("(p e) n -> p (e n)", e=PAIR),
+                in_=res[:].rearrange("p e n -> p (e n)"),
+            )

@@ -52,8 +52,8 @@ def tile_mix_outl_tm_res_kernel(
         nc.sync.dma_start(
             out=w8[:].bitcast(I32), in_=w8_words[0].rearrange("p n i -> p (n i)").bitcast(I32)
         )
-        nc.sync.dma_start(out=w4[:].bitcast(I32), in_=w4_words[0].bitcast(I32))
         load_x(1)
+        nc.sync.dma_start(out=w4[:].bitcast(I32), in_=w4_words[0].bitcast(I32))
         r_in = []
         for c in range(N_CHUNKS):
             rt = keep.tile([P, PAIR, N], F32, name="r%d" % c, align_bytes=64)
@@ -96,13 +96,18 @@ def tile_mix_outl_tm_res_kernel(
                 out=x_codes[g, c][:].bitcast(FP8X4), scales=x_planes[g, c][:], in_=grouped[g, c][:]
             )
 
-        for g in range(2):
+        def regroup_all(g):
             regroup(g, 0, nc.vector.tensor_copy)
             regroup(g, 2, nc.scalar.copy)
             regroup(g, 1, nc.vector.tensor_copy)
             regroup(g, 3, nc.scalar.copy)
-            for c in range(N_CHUNKS):
-                quantize(g, c)
+
+        regroup_all(0)
+        for c in range(N_CHUNKS):
+            quantize(0, c)
+        regroup_all(1)
+        for c in range(N_CHUNKS - 1):
+            quantize(1, c)
 
         banks = {}
 
@@ -145,6 +150,8 @@ def tile_mix_outl_tm_res_kernel(
                 nc.vector.tensor_add(
                     out=res[:, e, cols], in0=banks[c, e, h][:], in1=r_in[c][:, e, cols]
                 )
+            if c == 0:
+                quantize(1, N_CHUNKS - 1)
             nc.sync.dma_start(
                 out=out[c * CHUNK : (c + 1) * CHUNK, :].rearrange("(p e) n -> p (e n)", e=PAIR),
                 in_=res[:].rearrange("p e n -> p (e n)"),

from contextlib import ExitStack

import concourse.mybir as mybir

O, K, N, T = 512, 1024, 1024, 1024
FLOPS = 2 * K * N * T

F32 = mybir.dt.float32
BF16 = mybir.dt.bfloat16
I32 = mybir.dt.int32
U32 = mybir.dt.uint32
U8 = mybir.dt.uint8
FP8X4 = mybir.dt.float8_e4m3fn_x4
FP4X4 = mybir.dt.float4_e2m1fn_x4

P = 128
PACK = 4
K_PASS = P * PACK
PAIR = 2
CHUNK = PAIR * P
N_CHUNKS = T // CHUNK
N_BANK = 512
N_HALVES = N // N_BANK
Q_ROWS = 4


def tile_mix_outl_tm_res_kernel(
    tc, x, w8_words, w8_scales, w4_words, w4_scales, r, out
):
    nc = tc.nc
    with ExitStack() as ctx:
        keep = ctx.enter_context(tc.tile_pool(name="keep", bufs=1))
        psum = ctx.enter_context(tc.psum_pool(name="psum", bufs=8))
        ctx.enter_context(tc.manual_schedule())

        x_raw = []
        for g in range(K // K_PASS):
            raw = keep.tile([P, PACK, T], F32, name="x_raw%d" % g, align_bytes=64)
            x_raw.append(raw)
        w8 = keep.tile([P, 4 * N], U8, name="w8", align_bytes=64)
        w4 = keep.tile([P, 2 * N], U8, name="w4", align_bytes=64)
        w8_plane = keep.tile([P, N], U8, name="w8_plane", align_bytes=64)
        w4_plane = keep.tile([P, N], U8, name="w4_plane", align_bytes=64)

        def load_x(g):
            nc.sync.dma_start(
                out=x_raw[g][:].rearrange("p k t -> p (k t)"),
                in_=x[g * K_PASS : (g + 1) * K_PASS, :].rearrange("(p k) t -> p (k t)", k=PACK),
            )

        load_x(0)
        nc.sync.dma_start(
            out=w8[:].bitcast(I32), in_=w8_words[0].rearrange("p n i -> p (n i)").bitcast(I32)
        )
        load_x(1)
        nc.sync.dma_start(out=w4[:].bitcast(I32), in_=w4_words[0].bitcast(I32))
        r_in = []
        for c in range(N_CHUNKS):
            rt = keep.tile([P, PAIR, N], F32, name="r%d" % c, align_bytes=64)
            r_in.append(rt)
            nc.sync.dma_start(
                out=rt[:].rearrange("p e n -> p (e n)"),
                in_=r[c * CHUNK : (c + 1) * CHUNK, :].rearrange("(p e) n -> p (e n)", e=PAIR),
            )

        for plane, scales in ((w8_plane, w8_scales), (w4_plane, w4_scales)):
            nc.vector.memset(plane[:].bitcast(I32), 0)
            for q in range(P // 32):
                nc.gpsimd.dma_start(
                    out=plane[32 * q : 32 * q + Q_ROWS, :].bitcast(I32),
                    in_=scales[0, Q_ROWS * q : Q_ROWS * (q + 1), :].bitcast(I32),
                )

        x_codes = {}
        x_planes = {}
        grouped = {}
        for g in range(2):
            for c in range(N_CHUNKS):
                t_g = keep.tile([P, CHUNK * PACK], BF16, name="grouped%d_%d" % (g, c), align_bytes=64)
                t_c = keep.tile([P, CHUNK], U32, name="codes%d_%d" % (g, c), align_bytes=64)
                t_s = keep.tile([P, CHUNK], U8, name="xscale%d_%d" % (g, c), align_bytes=64)
                grouped[g, c] = t_g
                x_codes[g, c] = t_c
                x_planes[g, c] = t_s

        def regroup(g, c, copy):
            copy(
                out=grouped[g, c][:].rearrange("p (e m k) -> p e m k", e=PAIR, k=PACK),
                in_=x_raw[g][:, :, c * CHUNK : (c + 1) * CHUNK].rearrange(
                    "p k (m e) -> p e m k", e=PAIR
                ),
            )

        def quantize(g, c):
            nc.vector.quantize_mx(
                out=x_codes[g, c][:].bitcast(FP8X4), scales=x_planes[g, c][:], in_=grouped[g, c][:]
            )

        def regroup_all(g):
            regroup(g, 0, nc.vector.tensor_copy)
            regroup(g, 2, nc.scalar.copy)
            regroup(g, 1, nc.vector.tensor_copy)
            regroup(g, 3, nc.scalar.copy)

        regroup_all(0)
        for c in range(N_CHUNKS):
            quantize(0, c)
        regroup_all(1)
        for c in range(N_CHUNKS - 1):
            quantize(1, c)

        banks = {}

        def first_pass(c, e, h):
            acc = psum.tile([P, N_BANK], F32, name="acc")
            banks[c, e, h] = acc
            nc.tensor.matmul_mx(
                out=acc[:],
                lhsT=x_codes[0, c][:, e * P : (e + 1) * P].bitcast(FP8X4),
                lhsT_scale=x_planes[0, c][:, e * P : (e + 1) * P],
                rhs=w8[:, 4 * N_BANK * h : 4 * N_BANK * (h + 1)].bitcast(FP8X4),
                rhs_scale=w8_plane[:, N_BANK * h : N_BANK * (h + 1)],
                start=True,
                stop=False,
            )

        def second_pass(c, e, h):
            nc.tensor.matmul_mx(
                out=banks[c, e, h][:],
                lhsT=x_codes[1, c][:, e * P : (e + 1) * P].bitcast(FP8X4),
                lhsT_scale=x_planes[1, c][:, e * P : (e + 1) * P],
                rhs=w4[:, 2 * N_BANK * h : 2 * N_BANK * (h + 1)].bitcast(FP4X4),
                rhs_scale=w4_plane[:, N_BANK * h : N_BANK * (h + 1)],
                start=False,
                stop=True,
            )

        places = [(e, h) for e in range(PAIR) for h in range(N_HALVES)]
        for c in range(2):
            for e, h in places:
                first_pass(c, e, h)
        for c in range(N_CHUNKS):
            for e, h in places:
                if c >= 2:
                    first_pass(c, e, h)
                second_pass(c, e, h)
            res = keep.tile([P, PAIR, N], F32, name="res%d" % c, align_bytes=64)
            for e, h in places:
                cols = slice(N_BANK * h, N_BANK * (h + 1))
                nc.vector.tensor_add(
                    out=res[:, e, cols], in0=banks[c, e, h][:], in1=r_in[c][:, e, cols]
                )
            if c == 0:
                quantize(1, N_CHUNKS - 1)
            nc.sync.dma_start(
                out=out[c * CHUNK : (c + 1) * CHUNK, :].rearrange("(p e) n -> p (e n)", e=PAIR),
                in_=res[:].rearrange("p e n -> p (e n)"),
            )
